import numpy as np
import ml_dtypes


def mxq(x, axis, fmt="e4m3"):
    dtype, down = {"e4m3": (ml_dtypes.float8_e4m3fn, 7), "e5m2": (ml_dtypes.float8_e5m2, 14)}[fmt]
    v = np.moveaxis(np.asarray(x, np.float32).astype(ml_dtypes.bfloat16).astype(np.float64), axis, -1)
    blocks = v.reshape(v.shape[:-1] + (-1, 32))
    amax = np.abs(blocks).max(-1, keepdims=True)
    byte = np.maximum(np.where(amax > 0, np.frexp(amax)[1] - 1 + 127, 0) - down, 1)
    scale = np.exp2(byte - 127.0)
    codes = (blocks / scale).astype(np.float32).astype(dtype).astype(np.float64)
    return np.moveaxis((codes * scale).reshape(v.shape), -1, axis)


WIDE = False


def mx_kscale(k):
    if not WIDE:
        return np.ones(k)
    levels = np.array([10, -10, 5, -5, 0])
    if k % 512:
        return np.exp2(np.random.permutation(np.resize(levels, k // 32))).repeat(32)
    a = np.empty((k // 512, 16))
    for p in range(k // 512):
        a[p, :8] = np.random.permutation(np.resize(levels, 8))
        for g in range(8):
            far = levels[np.abs(levels - a[p, g]) >= 10]
            a[p, g + 8] = far[np.random.randint(len(far))]
    return np.exp2(a.ravel()).repeat(32)


def f64(x):
    return np.asarray(x).astype(np.float64)


E2M1 = np.array([0.0, 0.5, 1.0, 1.5, 2.0, 3.0, 4.0, 6.0, -0.0, -0.5, -1.0, -1.5, -2.0, -3.0, -4.0, -6.0])


def pack_weight(w, fmt):
    k, n = w.shape
    w = f64(np.asarray(w, np.float32).astype(ml_dtypes.bfloat16)).reshape(k // 32, 32, n)
    amax = np.abs(w).max(1)
    if fmt == "e4m3":
        byte = np.frexp(amax)[1] - 1 + 127 - 7
    else:
        mant, ex = np.frexp(amax / 6.0)
        byte = np.where(mant > 0.5, ex, ex - 1) + 127
    byte = np.clip(np.where(amax > 0, byte, 1), 1, 254)
    scaled = (w * np.exp2(127.0 - byte)[:, None, :]).reshape(k, n).astype(np.float32)
    by_word = np.ascontiguousarray(scaled.reshape(k // 512, 128, 4, n).transpose(0, 1, 3, 2))
    if fmt == "e4m3":
        words = by_word.astype(ml_dtypes.float8_e4m3fn).view(np.uint8)
    else:
        c = by_word.astype(ml_dtypes.float4_e2m1fn).view(np.uint8) & 0xF
        words = (c[..., 0::2] | (c[..., 1::2] << 4)).reshape(k // 512, 128, 2 * n)
    return np.ascontiguousarray(words), np.ascontiguousarray(byte.astype(np.uint8).reshape(k // 512, 16, n))


def unpack_weight(words, scales, fmt):
    g, _, n = scales.shape
    words = np.ascontiguousarray(words).reshape(g, 128, n, -1)
    if fmt == "e4m3":
        vals = words.view(ml_dtypes.float8_e4m3fn).astype(np.float64)
    else:
        nib = np.empty((g, 128, n, 4), np.uint8)
        nib[..., 0::2] = words & 0xF
        nib[..., 1::2] = words >> 4
        vals = E2M1[nib]
    vals = vals * np.repeat(np.exp2(scales.astype(np.float64) - 127.0), 8, axis=1)[..., None]
    return vals.transpose(0, 1, 3, 2).reshape(g * 512, n)


def silu(v):
    return v / (1.0 + np.exp(-np.maximum(v, -700.0)))


K, M, T = 1536, 1024, 1536


def setup_inputs():
    n = np.random.standard_normal
    s = mx_kscale(K)[:, None]
    p_w4 = pack_weight(n((K, M)) / np.sqrt(K) / s ** 2, "e2m1")
    p_w8 = pack_weight(n((K, M)) / np.sqrt(K) / s, "e4m3")
    return {
        "x": (n((K, T)) * s).astype(np.float32),
        "w4_words": p_w4[0],
        "w4_scales": p_w4[1],
        "w8_words": p_w8[0],
        "w8_scales": p_w8[1],
        "b": (0.3 * n(1024)).astype(np.float32),
    }


def reference(x, w4_words, w4_scales, w8_words, w8_scales, b):
    xa_, xb_ = mxq(f64(x) ** 2, 0, "e4m3"), mxq(f64(x), 0, "e4m3")
    w4_ = unpack_weight(w4_words, w4_scales, "e2m1")
    w8_ = unpack_weight(w8_words, w8_scales, "e4m3")
    y = w4_.T @ xa_ + w8_.T @ xb_
    return silu(y + f64(b)[:, None])

@@ -1,0 +1,238 @@
+from contextlib import ExitStack
+
+import concourse.mybir as mybir
+
+K, M, T = 1536, 1024, 1536
+FLOPS = 2 * 2 * K * M * T
+
+F32 = mybir.dt.float32
+BF16 = mybir.dt.bfloat16
+I32 = mybir.dt.int32
+U32 = mybir.dt.uint32
+U8 = mybir.dt.uint8
+FP8X4 = mybir.dt.float8_e4m3fn_x4
+FP4X4 = mybir.dt.float4_e2m1fn_x4
+ACT = mybir.ActivationFunctionType
+ALU = mybir.AluOpType
+
+P = 128
+PACK = 4
+K_PASS = P * PACK
+PASSES = K // K_PASS
+N_TILE = 512
+HALF = N_TILE // 2
+CHUNKS = T // N_TILE
+M_TILES = M // P
+RUN = 4
+HALVED = PASSES + 1
+LAG_CLOSE = 4
+LAG_OPEN = 5
+
+
+def tile_mix_feat_fm_quad_silu_kernel(tc, x, w4_words, w4_scales, w8_words, w8_scales, b, out):
+    nc = tc.nc
+    with ExitStack() as ctx:
+        keep = ctx.enter_context(tc.tile_pool(name="keep", bufs=1))
+        stage = ctx.enter_context(tc.tile_pool(name="stage", bufs=1))
+        psum = ctx.enter_context(tc.psum_pool(name="psum", bufs=1))
+        ctx.enter_context(tc.manual_schedule())
+
+        plane8 = keep.tile([P, PASSES, M], U8, align_bytes=64)
+        plane4 = keep.tile([P, PASSES, M], U8, align_bytes=64)
+        zero = keep.tile([P, 1], F32)
+        bias_rows = keep.tile([P, 32], F32, align_bytes=64)
+        bias = keep.tile([P, 32], F32, align_bytes=64)
+        nc.vector.memset(zero[:], 0.0)
+        nc.vector.memset(plane8[:].bitcast(I32), 0)
+        nc.vector.memset(plane4[:].bitcast(I32), 0)
+        nc.scalar.activation(out=bias_rows[:], in_=zero[:].to_broadcast([P, 32]), func=ACT.Silu)
+
+        tiles = [(c, a) for c in range(CHUNKS) for a in range(PASSES)]
+        raw = {}
+        w8 = {}
+        w4 = {}
+
+        def pieces(i):
+            return [(0, HALF), (HALF, HALF)] if i < HALVED else [(0, N_TILE)]
+
+        def load_x(i, c0, width):
+            c, a = tiles[i]
+            piece = keep.tile([P, PACK, width], F32, name="raw%d_%d" % (i, c0), align_bytes=64)
+            t0 = c * N_TILE + c0
+            rows = x[a * K_PASS : (a + 1) * K_PASS, t0 : t0 + width]
+            nc.sync.dma_start(out=piece[:], in_=rows.rearrange("(p j) t -> p j t", j=PACK))
+            raw[i, c0] = piece
+
+        def load_w8(a):
+            words = keep.tile([P, M], U32, name="w8_%d" % a, align_bytes=64)
+            nc.sync.dma_start(out=words[:].bitcast(I32), in_=w8_words[a].rearrange("p n i -> p (n i)").bitcast(I32))
+            w8[a] = words
+
+        def load_w4(a):
+            words = keep.tile([P, 2 * M], U8, name="w4_%d" % a, align_bytes=64)
+            nc.sync.dma_start(out=words[:].bitcast(I32), in_=w4_words[a].bitcast(I32))
+            w4[a] = words
+
+        def load_scales(plane, scales):
+            for r in range(4):
+                nc.sync.dma_start(
+                    out=plane[r:P:32, :, :].bitcast(I32),
+                    in_=scales[:, r:16:4, :].rearrange("a q n -> q a n").bitcast(I32),
+                )
+
+        for a in range(PASSES):
+            load_x(a, 0, HALF)
+            if a == 0:
+                load_scales(plane8, w8_scales)
+            load_w8(a)
+            load_x(a, HALF, HALF)
+            load_w4(a)
+            if a == 0:
+                load_scales(plane4, w4_scales)
+        nc.sync.dma_start(out=bias_rows[0:P:4, :], in_=b.rearrange("(m q j) -> q m j", q=4, j=32))
+        for i in range(PASSES, len(tiles)):
+            for c0, width in pieces(i):
+                load_x(i, c0, width)
+
+        codes = {}
+        scale = {}
+        grouped = {}
+        for i in range(len(tiles)):
+            for kind in ("xa", "xb"):
+                codes[kind, i] = keep.tile([P, N_TILE], U32, name="codes_%s%d" % (kind, i), align_bytes=64)
+                scale[kind, i] = keep.tile([P, N_TILE], U8, name="scale_%s%d" % (kind, i), align_bytes=64)
+
+        def views(kind, i, c0, width):
+            dst = stage.tile([P, width, PACK], BF16, name="g_%s%d_%d" % (kind, i, c0), tag="g_" + kind, bufs=4 if kind == "xa" else 3, align_bytes=64)
+            grouped[kind, i, c0] = dst
+            return (
+                dst[:].rearrange("p (c e) j -> p c j e", e=RUN),
+                raw[i, c0][:].rearrange("p j (c e) -> p c j e", e=RUN),
+            )
+
+        def cast(i, c0, width):
+            dst, src = views("xb", i, c0, width)
+            nc.vector.tensor_copy(out=dst, in_=src)
+
+        def square_scalar(i, c0, width):
+            dst, src = views("xa", i, c0, width)
+            nc.scalar.activation(out=dst, in_=src, func=ACT.Square)
+
+        def square_vector(i, c0, width):
+            dst, src = views("xa", i, c0, width)
+            nc.vector.tensor_tensor(out=dst, in0=src, in1=src, op=ALU.mult)
+
+        def quantize(kind, i, c0, width):
+            nc.vector.quantize_mx(
+                out=codes[kind, i][:, c0 : c0 + width].bitcast(FP8X4),
+                scales=scale[kind, i][:, c0 : c0 + width],
+                in_=grouped[kind, i, c0][:].rearrange("p t j -> p (t j)"),
+            )
+
+        acc = {}
+        result = {}
+
+        def linear(i, m, c0=0, width=N_TILE):
+            c, a = tiles[i]
+            first = a == 0 and c0 == 0
+            if first:
+                acc[c, m] = psum.tile([P, N_TILE], F32, name="acc%d_%d" % (c, m), tag="bank%d" % m)
+            cols = slice(c0, c0 + width)
+            nc.tensor.matmul_mx(
+                out=acc[c, m][:, cols],
+                lhsT=w8[a][:, m * P : (m + 1) * P].bitcast(FP8X4),
+                lhsT_scale=plane8[:, a, m * P : (m + 1) * P],
+                rhs=codes["xb", i][:, cols].bitcast(FP8X4),
+                rhs_scale=scale["xb", i][:, cols],
+                start=first,
+                stop=False,
+            )
+
+        def quadratic(i, m):
+            c, a = tiles[i]
+            nc.tensor.matmul_mx(
+                out=acc[c, m][:],
+                lhsT=w4[a][:, 2 * m * P : 2 * (m + 1) * P].bitcast(FP4X4),
+                lhsT_scale=plane4[:, a, m * P : (m + 1) * P],
+                rhs=codes["xa", i][:].bitcast(FP8X4),
+                rhs_scale=scale["xa", i][:],
+                start=False,
+                stop=(a == PASSES - 1),
+            )
+
+        def multiply(i, lag, c0=0, width=N_TILE, before=None, after=None):
+            for s in range(M_TILES + lag):
+                if s >= lag:
+                    quadratic(i, s - lag)
+                    if after is not None:
+                        after(s - lag)
+                if s < M_TILES:
+                    if before is not None:
+                        before(s)
+                    linear(i, s, c0, width)
+
+        def silu(c, m):
+            if m == 0:
+                result[c] = keep.tile([P, M_TILES, N_TILE], F32, name="result%d" % c)
+            nc.scalar.activation(out=result[c][:, m, :], in_=acc[c, m][:], func=ACT.Silu, bias=bias[:, 4 * m : 4 * m + 1])
+
+        def store(c, m0, count):
+            dst = out[m0 * P : (m0 + count) * P, c * N_TILE : (c + 1) * N_TILE]
+            nc.sync.dma_start(out=dst.rearrange("(m p) t -> p m t", p=P), in_=result[c][:, m0 : m0 + count, :])
+
+        def finish(c, m):
+            silu(c, m)
+            if c == CHUNKS - 1:
+                store(c, m, 1)
+            elif m % 4 == 3:
+                store(c, m - 3, 4)
+
+        for i in range(PASSES):
+            square_scalar(i, 0, HALF)
+            square_scalar(i, HALF, HALF)
+            cast(i, 0, HALF)
+            quantize("xb", i, 0, HALF)
+            cast(i, HALF, HALF)
+            quantize("xa", i, 0, HALF)
+            quantize("xb", i, HALF, HALF)
+            quantize("xa", i, HALF, HALF)
+            for m in range(M_TILES):
+                linear(i, m, 0, HALF)
+            multiply(i, M_TILES if i < PASSES - 1 else LAG_CLOSE, HALF, HALF)
+        nc.vector.transpose(bias[:], bias_rows[:])
+
+        square_scalar(3, 0, HALF)
+        cast(3, 0, HALF)
+        quantize("xb", 3, 0, HALF)
+        cast(3, HALF, HALF)
+        quantize("xa", 3, 0, HALF)
+        quantize("xb", 3, HALF, HALF)
+        square_vector(3, HALF, HALF)
+        cast(4, 0, N_TILE)
+        quantize("xa", 3, HALF, HALF)
+        quantize("xb", 4, 0, N_TILE)
+        multiply(3, LAG_OPEN, before=lambda m: finish(0, m))
+
+        square_scalar(4, 0, N_TILE)
+        square_scalar(5, 0, N_TILE)
+        cast(5, 0, N_TILE)
+        quantize("xa", 4, 0, N_TILE)
+        quantize("xb", 5, 0, N_TILE)
+        multiply(4, M_TILES)
+        cast(6, 0, N_TILE)
+        quantize("xa", 5, 0, N_TILE)
+        quantize("xb", 6, 0, N_TILE)
+        multiply(5, 1, after=lambda m: finish(1, m))
+        square_vector(6, 0, N_TILE)
+        cast(7, 0, N_TILE)
+        quantize("xa", 6, 0, N_TILE)
+        quantize("xb", 7, 0, N_TILE)
+        multiply(6, M_TILES)
+        square_scalar(7, 0, N_TILE)
+        square_scalar(8, 0, N_TILE)
+        cast(8, 0, N_TILE)
+        quantize("xa", 7, 0, N_TILE)
+        quantize("xb", 8, 0, N_TILE)
+        multiply(7, M_TILES)
+        quantize("xa", 8, 0, N_TILE)
+        multiply(8, 1, after=lambda m: finish(2, m))

@@ -24,7 +24,9 @@ HALF = N_TILE // 2
 CHUNKS = T // N_TILE
 M_TILES = M // P
 RUN = 4
-HALVED = PASSES + 1
+HALVED = (0, 3)
+EARLY = True
+LAG = 2
 LAG_CLOSE = 4
 LAG_OPEN = 5
 
@@ -37,13 +39,18 @@ def tile_mix_feat_fm_quad_silu_kernel(tc, x, w4_words, w4_scales, w8_words, w8_s
         psum = ctx.enter_context(tc.psum_pool(name="psum", bufs=1))
         ctx.enter_context(tc.manual_schedule())
 
-        plane8 = keep.tile([P, PASSES, M], U8, align_bytes=64)
+        plane8 = keep.tile([P, M], U8, align_bytes=64)
         plane4 = keep.tile([P, PASSES, M], U8, align_bytes=64)
         zero = keep.tile([P, 1], F32)
         bias_rows = keep.tile([P, 32], F32, align_bytes=64)
         bias = keep.tile([P, 32], F32, align_bytes=64)
-        nc.vector.memset(zero[:], 0.0)
         nc.vector.memset(plane8[:].bitcast(I32), 0)
+        nc.vector.memset(zero[:], 0.0)
+        for q in range(4):
+            nc.scalar.dma_start(
+                out=plane8[32 * q + 4 : 32 * q + 16, :].bitcast(I32),
+                in_=w8_scales[:, 4 * q : 4 * q + 4, :].bitcast(I32),
+            )
         nc.vector.memset(plane4[:].bitcast(I32), 0)
         nc.scalar.activation(out=bias_rows[:], in_=zero[:].to_broadcast([P, 32]), func=ACT.Silu)
 
@@ -53,7 +60,7 @@ def tile_mix_feat_fm_quad_silu_kernel(tc, x, w4_words, w4_scales, w8_words, w8_s
         w4 = {}
 
         def pieces(i):
-            return [(0, HALF), (HALF, HALF)] if i < HALVED else [(0, N_TILE)]
+            return [(0, HALF), (HALF, HALF)] if i in HALVED else [(0, N_TILE)]
 
         def load_x(i, c0, width):
             c, a = tiles[i]
@@ -81,18 +88,20 @@ def tile_mix_feat_fm_quad_silu_kernel(tc, x, w4_words, w4_scales, w8_words, w8_s
                 )
 
         for a in range(PASSES):
-            load_x(a, 0, HALF)
-            if a == 0:
-                load_scales(plane8, w8_scales)
+            load_x(a, *pieces(a)[0])
             load_w8(a)
-            load_x(a, HALF, HALF)
+            for piece in pieces(a)[1:]:
+                load_x(a, *piece)
+            if a == PASSES - 1 and EARLY:
+                load_x(PASSES, *pieces(PASSES)[0])
             load_w4(a)
             if a == 0:
                 load_scales(plane4, w4_scales)
         nc.sync.dma_start(out=bias_rows[0:P:4, :], in_=b.rearrange("(m q j) -> q m j", q=4, j=32))
         for i in range(PASSES, len(tiles)):
             for c0, width in pieces(i):
-                load_x(i, c0, width)
+                if (i, c0) not in raw:
+                    load_x(i, c0, width)
 
         codes = {}
         scale = {}
@@ -103,11 +112,12 @@ def tile_mix_feat_fm_quad_silu_kernel(tc, x, w4_words, w4_scales, w8_words, w8_s
                 scale[kind, i] = keep.tile([P, N_TILE], U8, name="scale_%s%d" % (kind, i), align_bytes=64)
 
         def views(kind, i, c0, width):
-            dst = stage.tile([P, width, PACK], BF16, name="g_%s%d_%d" % (kind, i, c0), tag="g_" + kind, bufs=4 if kind == "xa" else 3, align_bytes=64)
+            dst = stage.tile([P, width, PACK], BF16, name="g_%s%d_%d" % (kind, i, c0), tag="g_" + kind, bufs=5 if kind == "xa" else 3, align_bytes=64)
             grouped[kind, i, c0] = dst
+            src = raw[i, c0][:] if i in HALVED else raw[i, 0][:, :, c0 : c0 + width]
             return (
                 dst[:].rearrange("p (c e) j -> p c j e", e=RUN),
-                raw[i, c0][:].rearrange("p j (c e) -> p c j e", e=RUN),
+                src.rearrange("p j (c e) -> p c j e", e=RUN),
             )
 
         def cast(i, c0, width):
@@ -121,6 +131,16 @@ def tile_mix_feat_fm_quad_silu_kernel(tc, x, w4_words, w4_scales, w8_words, w8_s
         def square_vector(i, c0, width):
             dst, src = views("xa", i, c0, width)
             nc.vector.tensor_tensor(out=dst, in0=src, in1=src, op=ALU.mult)
+
+        def square_flat(i, c0, width):
+            flat = stage.tile([P, PACK, width], BF16, name="flat%d_%d" % (i, c0), tag="flat", bufs=2, align_bytes=64)
+            src = raw[i, 0][:, :, c0 : c0 + width]
+            nc.vector.tensor_tensor(out=flat[:], in0=src, in1=src, op=ALU.mult)
+            raw["flat", i] = flat
+
+        def interleave_flat(i, c0, width):
+            dst = views("xa", i, c0, width)[0]
+            nc.vector.tensor_copy(out=dst, in_=raw["flat", i][:].rearrange("p j (c e) -> p c j e", e=RUN))
 
         def quantize(kind, i, c0, width):
             nc.vector.quantize_mx(
@@ -141,7 +161,7 @@ def tile_mix_feat_fm_quad_silu_kernel(tc, x, w4_words, w4_scales, w8_words, w8_s
             nc.tensor.matmul_mx(
                 out=acc[c, m][:, cols],
                 lhsT=w8[a][:, m * P : (m + 1) * P].bitcast(FP8X4),
-                lhsT_scale=plane8[:, a, m * P : (m + 1) * P],
+                lhsT_scale=plane8[4 * (a + 1) :, m * P : (m + 1) * P],
                 rhs=codes["xb", i][:, cols].bitcast(FP8X4),
                 rhs_scale=scale["xb", i][:, cols],
                 start=first,
@@ -187,6 +207,14 @@ def tile_mix_feat_fm_quad_silu_kernel(tc, x, w4_words, w4_scales, w8_words, w8_s
             elif m % 4 == 3:
                 store(c, m - 3, 4)
 
+        def linears(i, c0=0, width=N_TILE):
+            for m in range(M_TILES):
+                linear(i, m, c0, width)
+
+        def quadratics(i):
+            for m in range(M_TILES):
+                quadratic(i, m)
+
         for i in range(PASSES):
             square_scalar(i, 0, HALF)
             square_scalar(i, HALF, HALF)
@@ -196,43 +224,54 @@ def tile_mix_feat_fm_quad_silu_kernel(tc, x, w4_words, w4_scales, w8_words, w8_s
             quantize("xa", i, 0, HALF)
             quantize("xb", i, HALF, HALF)
             quantize("xa", i, HALF, HALF)
-            for m in range(M_TILES):
-                linear(i, m, 0, HALF)
-            multiply(i, M_TILES if i < PASSES - 1 else LAG_CLOSE, HALF, HALF)
+            linears(i, 0, HALF)
+            if i < PASSES - 1:
+                linears(i, HALF, HALF)
+                quadratics(i)
         nc.vector.transpose(bias[:], bias_rows[:])
-
         square_scalar(3, 0, HALF)
         cast(3, 0, HALF)
         quantize("xb", 3, 0, HALF)
         cast(3, HALF, HALF)
         quantize("xa", 3, 0, HALF)
         quantize("xb", 3, HALF, HALF)
-        square_vector(3, HALF, HALF)
-        cast(4, 0, N_TILE)
-        quantize("xa", 3, HALF, HALF)
-        quantize("xb", 4, 0, N_TILE)
-        multiply(3, LAG_OPEN, before=lambda m: finish(0, m))
-
-        square_scalar(4, 0, N_TILE)
+        multiply(2, LAG_CLOSE, HALF, HALF, after=lambda m: finish(0, m))
+        linears(3)
+        square_scalar(3, HALF, HALF)
+        square_scalar(4, 0, HALF)
         square_scalar(5, 0, N_TILE)
+        cast(4, 0, N_TILE)
+        quantize("xb", 4, 0, N_TILE)
+        square_flat(4, HALF, HALF)
+        quantize("xa", 3, HALF, HALF)
+        interleave_flat(4, HALF, HALF)
         cast(5, 0, N_TILE)
-        quantize("xa", 4, 0, N_TILE)
+        quantize("xa", 4, HALF, HALF)
+        quantize("xa", 4, 0, HALF)
         quantize("xb", 5, 0, N_TILE)
-        multiply(4, M_TILES)
-        cast(6, 0, N_TILE)
         quantize("xa", 5, 0, N_TILE)
-        quantize("xb", 6, 0, N_TILE)
+        cast(6, 0, N_TILE)
+        linears(4)
+        quadratics(3)
+        quadratics(4)
         multiply(5, 1, after=lambda m: finish(1, m))
-        square_vector(6, 0, N_TILE)
-        cast(7, 0, N_TILE)
+        square_flat(6, 0, N_TILE)
+        quantize("xb", 6, 0, N_TILE)
+        interleave_flat(6, 0, N_TILE)
         quantize("xa", 6, 0, N_TILE)
+        cast(7, 0, N_TILE)
         quantize("xb", 7, 0, N_TILE)
-        multiply(6, M_TILES)
         square_scalar(7, 0, N_TILE)
         square_scalar(8, 0, N_TILE)
         cast(8, 0, N_TILE)
         quantize("xa", 7, 0, N_TILE)
         quantize("xb", 8, 0, N_TILE)
-        multiply(7, M_TILES)
         quantize("xa", 8, 0, N_TILE)
-        multiply(8, 1, after=lambda m: finish(2, m))
+        linears(6)
+        quadratics(6)
+        linears(7)
+        for m in range(M_TILES):
+            quadratic(7, m)
+            linear(8, m)
+            quadratic(8, m)
+            finish(2, m)

@@ -39,19 +39,16 @@ def tile_mix_feat_fm_quad_silu_kernel(tc, x, w4_words, w4_scales, w8_words, w8_s
         psum = ctx.enter_context(tc.psum_pool(name="psum", bufs=1))
         ctx.enter_context(tc.manual_schedule())
 
-        plane8 = keep.tile([P, M], U8, align_bytes=64)
-        plane4 = keep.tile([P, PASSES, M], U8, align_bytes=64)
+        plane8 = keep.tile([P, 1, M], U8, align_bytes=256)
+        plane8_rest = keep.tile([P, PASSES - 1, M], U8, align_bytes=256)
+        plane4 = keep.tile([P, PASSES, M], U8, align_bytes=256)
         zero = keep.tile([P, 1], F32)
         bias_rows = keep.tile([P, 32], F32, align_bytes=64)
         bias = keep.tile([P, 32], F32, align_bytes=64)
         nc.vector.memset(plane8[:].bitcast(I32), 0)
         nc.vector.memset(zero[:], 0.0)
-        for q in range(4):
-            nc.scalar.dma_start(
-                out=plane8[32 * q + 4 : 32 * q + 16, :].bitcast(I32),
-                in_=w8_scales[:, 4 * q : 4 * q + 4, :].bitcast(I32),
-            )
         nc.vector.memset(plane4[:].bitcast(I32), 0)
+        nc.vector.memset(plane8_rest[:].bitcast(I32), 0)
         nc.scalar.activation(out=bias_rows[:], in_=zero[:].to_broadcast([P, 32]), func=ACT.Silu)
 
         tiles = [(c, a) for c in range(CHUNKS) for a in range(PASSES)]
@@ -71,12 +68,12 @@ def tile_mix_feat_fm_quad_silu_kernel(tc, x, w4_words, w4_scales, w8_words, w8_s
             raw[i, c0] = piece
 
         def load_w8(a):
-            words = keep.tile([P, M], U32, name="w8_%d" % a, align_bytes=64)
+            words = keep.tile([P, M], U32, name="w8_%d" % a, align_bytes=256)
             nc.sync.dma_start(out=words[:].bitcast(I32), in_=w8_words[a].rearrange("p n i -> p (n i)").bitcast(I32))
             w8[a] = words
 
         def load_w4(a):
-            words = keep.tile([P, 2 * M], U8, name="w4_%d" % a, align_bytes=64)
+            words = keep.tile([P, 2 * M], U8, name="w4_%d" % a, align_bytes=256)
             nc.sync.dma_start(out=words[:].bitcast(I32), in_=w4_words[a].bitcast(I32))
             w4[a] = words
 
@@ -89,7 +86,11 @@ def tile_mix_feat_fm_quad_silu_kernel(tc, x, w4_words, w4_scales, w8_words, w8_s
 
         for a in range(PASSES):
             load_x(a, *pieces(a)[0])
+            if a == 1:
+                load_scales(plane8_rest, w8_scales[1:])
             load_w8(a)
+            if a == 0:
+                load_scales(plane8, w8_scales[0:1])
             for piece in pieces(a)[1:]:
                 load_x(a, *piece)
             if a == PASSES - 1 and EARLY:
@@ -108,8 +109,8 @@ def tile_mix_feat_fm_quad_silu_kernel(tc, x, w4_words, w4_scales, w8_words, w8_s
         grouped = {}
         for i in range(len(tiles)):
             for kind in ("xa", "xb"):
-                codes[kind, i] = keep.tile([P, N_TILE], U32, name="codes_%s%d" % (kind, i), align_bytes=64)
-                scale[kind, i] = keep.tile([P, N_TILE], U8, name="scale_%s%d" % (kind, i), align_bytes=64)
+                codes[kind, i] = keep.tile([P, N_TILE], U32, name="codes_%s%d" % (kind, i), align_bytes=256)
+                scale[kind, i] = keep.tile([P, N_TILE], U8, name="scale_%s%d" % (kind, i), align_bytes=256)
 
         def views(kind, i, c0, width):
             dst = stage.tile([P, width, PACK], BF16, name="g_%s%d_%d" % (kind, i, c0), tag="g_" + kind, bufs=5 if kind == "xa" else 3, align_bytes=64)
@@ -161,7 +162,7 @@ def tile_mix_feat_fm_quad_silu_kernel(tc, x, w4_words, w4_scales, w8_words, w8_s
             nc.tensor.matmul_mx(
                 out=acc[c, m][:, cols],
                 lhsT=w8[a][:, m * P : (m + 1) * P].bitcast(FP8X4),
-                lhsT_scale=plane8[4 * (a + 1) :, m * P : (m + 1) * P],
+                lhsT_scale=plane8_rest[:, a - 1, m * P : (m + 1) * P] if a else plane8[:, 0, m * P : (m + 1) * P],
                 rhs=codes["xb", i][:, cols].bitcast(FP8X4),
                 rhs_scale=scale["xb", i][:, cols],
                 start=first,

from contextlib import ExitStack

import concourse.mybir as mybir

K, M, T = 1536, 1024, 1536
FLOPS = 2 * 2 * K * M * T

F32 = mybir.dt.float32
BF16 = mybir.dt.bfloat16
I32 = mybir.dt.int32
U32 = mybir.dt.uint32
U8 = mybir.dt.uint8
FP8X4 = mybir.dt.float8_e4m3fn_x4
FP4X4 = mybir.dt.float4_e2m1fn_x4
ACT = mybir.ActivationFunctionType
ALU = mybir.AluOpType

P = 128
PACK = 4
K_PASS = P * PACK
PASSES = K // K_PASS
N_TILE = 512
HALF = N_TILE // 2
CHUNKS = T // N_TILE
M_TILES = M // P
RUN = 4
HALVED = (0, 3)
EARLY = True
LAG = 2
LAG_CLOSE = 4
LAG_OPEN = 5


def tile_mix_feat_fm_quad_silu_kernel(tc, x, w4_words, w4_scales, w8_words, w8_scales, b, out):
    nc = tc.nc
    with ExitStack() as ctx:
        keep = ctx.enter_context(tc.tile_pool(name="keep", bufs=1))
        stage = ctx.enter_context(tc.tile_pool(name="stage", bufs=1))
        psum = ctx.enter_context(tc.psum_pool(name="psum", bufs=1))
        ctx.enter_context(tc.manual_schedule())

        plane8 = keep.tile([P, 1, M], U8, align_bytes=256)
        plane8_rest = keep.tile([P, PASSES - 1, M], U8, align_bytes=256)
        plane4 = keep.tile([P, PASSES, M], U8, align_bytes=256)
        zero = keep.tile([P, 1], F32)
        bias_rows = keep.tile([P, 32], F32, align_bytes=64)
        bias = keep.tile([P, 32], F32, align_bytes=64)
        nc.vector.memset(plane8[:].bitcast(I32), 0)
        nc.vector.memset(zero[:], 0.0)
        nc.vector.memset(plane4[:].bitcast(I32), 0)
        nc.vector.memset(plane8_rest[:].bitcast(I32), 0)
        nc.scalar.activation(out=bias_rows[:], in_=zero[:].to_broadcast([P, 32]), func=ACT.Silu)

        tiles = [(c, a) for c in range(CHUNKS) for a in range(PASSES)]
        raw = {}
        w8 = {}
        w4 = {}

        def pieces(i):
            return [(0, HALF), (HALF, HALF)] if i in HALVED else [(0, N_TILE)]

        def load_x(i, c0, width):
            c, a = tiles[i]
            piece = keep.tile([P, PACK, width], F32, name="raw%d_%d" % (i, c0), align_bytes=64)
            t0 = c * N_TILE + c0
            rows = x[a * K_PASS : (a + 1) * K_PASS, t0 : t0 + width]
            nc.sync.dma_start(out=piece[:], in_=rows.rearrange("(p j) t -> p j t", j=PACK))
            raw[i, c0] = piece

        def load_w8(a):
            words = keep.tile([P, M], U32, name="w8_%d" % a, align_bytes=256)
            nc.sync.dma_start(out=words[:].bitcast(I32), in_=w8_words[a].rearrange("p n i -> p (n i)").bitcast(I32))
            w8[a] = words

        def load_w4(a):
            words = keep.tile([P, 2 * M], U8, name="w4_%d" % a, align_bytes=256)
            nc.sync.dma_start(out=words[:].bitcast(I32), in_=w4_words[a].bitcast(I32))
            w4[a] = words

        def load_scales(plane, scales):
            for r in range(4):
                nc.sync.dma_start(
                    out=plane[r:P:32, :, :].bitcast(I32),
                    in_=scales[:, r:16:4, :].rearrange("a q n -> q a n").bitcast(I32),
                )

        for a in range(PASSES):
            load_x(a, *pieces(a)[0])
            if a == 1:
                load_scales(plane8_rest, w8_scales[1:])
            load_w8(a)
            if a == 0:
                load_scales(plane8, w8_scales[0:1])
            for piece in pieces(a)[1:]:
                load_x(a, *piece)
            if a == PASSES - 1 and EARLY:
                load_x(PASSES, *pieces(PASSES)[0])
            load_w4(a)
            if a == 0:
                load_scales(plane4, w4_scales)
        nc.sync.dma_start(out=bias_rows[0:P:4, :], in_=b.rearrange("(m q j) -> q m j", q=4, j=32))
        for i in range(PASSES, len(tiles)):
            for c0, width in pieces(i):
                if (i, c0) not in raw:
                    load_x(i, c0, width)

        codes = {}
        scale = {}
        grouped = {}
        for i in range(len(tiles)):
            for kind in ("xa", "xb"):
                codes[kind, i] = keep.tile([P, N_TILE], U32, name="codes_%s%d" % (kind, i), align_bytes=256)
                scale[kind, i] = keep.tile([P, N_TILE], U8, name="scale_%s%d" % (kind, i), align_bytes=256)

        def views(kind, i, c0, width):
            dst = stage.tile([P, width, PACK], BF16, name="g_%s%d_%d" % (kind, i, c0), tag="g_" + kind, bufs=5 if kind == "xa" else 3, align_bytes=64)
            grouped[kind, i, c0] = dst
            src = raw[i, c0][:] if i in HALVED else raw[i, 0][:, :, c0 : c0 + width]
            return (
                dst[:].rearrange("p (c e) j -> p c j e", e=RUN),
                src.rearrange("p j (c e) -> p c j e", e=RUN),
            )

        def cast(i, c0, width):
            dst, src = views("xb", i, c0, width)
            nc.vector.tensor_copy(out=dst, in_=src)

        def square_scalar(i, c0, width):
            dst, src = views("xa", i, c0, width)
            nc.scalar.activation(out=dst, in_=src, func=ACT.Square)

        def square_vector(i, c0, width):
            dst, src = views("xa", i, c0, width)
            nc.vector.tensor_tensor(out=dst, in0=src, in1=src, op=ALU.mult)

        def square_flat(i, c0, width):
            flat = stage.tile([P, PACK, width], BF16, name="flat%d_%d" % (i, c0), tag="flat", bufs=2, align_bytes=64)
            src = raw[i, 0][:, :, c0 : c0 + width]
            nc.vector.tensor_tensor(out=flat[:], in0=src, in1=src, op=ALU.mult)
            raw["flat", i] = flat

        def interleave_flat(i, c0, width):
            dst = views("xa", i, c0, width)[0]
            nc.vector.tensor_copy(out=dst, in_=raw["flat", i][:].rearrange("p j (c e) -> p c j e", e=RUN))

        def quantize(kind, i, c0, width):
            nc.vector.quantize_mx(
                out=codes[kind, i][:, c0 : c0 + width].bitcast(FP8X4),
                scales=scale[kind, i][:, c0 : c0 + width],
                in_=grouped[kind, i, c0][:].rearrange("p t j -> p (t j)"),
            )

        acc = {}
        result = {}

        def linear(i, m, c0=0, width=N_TILE):
            c, a = tiles[i]
            first = a == 0 and c0 == 0
            if first:
                acc[c, m] = psum.tile([P, N_TILE], F32, name="acc%d_%d" % (c, m), tag="bank%d" % m)
            cols = slice(c0, c0 + width)
            nc.tensor.matmul_mx(
                out=acc[c, m][:, cols],
                lhsT=w8[a][:, m * P : (m + 1) * P].bitcast(FP8X4),
                lhsT_scale=plane8_rest[:, a - 1, m * P : (m + 1) * P] if a else plane8[:, 0, m * P : (m + 1) * P],
                rhs=codes["xb", i][:, cols].bitcast(FP8X4),
                rhs_scale=scale["xb", i][:, cols],
                start=first,
                stop=False,
            )

        def quadratic(i, m):
            c, a = tiles[i]
            nc.tensor.matmul_mx(
                out=acc[c, m][:],
                lhsT=w4[a][:, 2 * m * P : 2 * (m + 1) * P].bitcast(FP4X4),
                lhsT_scale=plane4[:, a, m * P : (m + 1) * P],
                rhs=codes["xa", i][:].bitcast(FP8X4),
                rhs_scale=scale["xa", i][:],
                start=False,
                stop=(a == PASSES - 1),
            )

        def multiply(i, lag, c0=0, width=N_TILE, before=None, after=None):
            for s in range(M_TILES + lag):
                if s >= lag:
                    quadratic(i, s - lag)
                    if after is not None:
                        after(s - lag)
                if s < M_TILES:
                    if before is not None:
                        before(s)
                    linear(i, s, c0, width)

        def silu(c, m):
            if m == 0:
                result[c] = keep.tile([P, M_TILES, N_TILE], F32, name="result%d" % c)
            nc.scalar.activation(out=result[c][:, m, :], in_=acc[c, m][:], func=ACT.Silu, bias=bias[:, 4 * m : 4 * m + 1])

        def store(c, m0, count):
            dst = out[m0 * P : (m0 + count) * P, c * N_TILE : (c + 1) * N_TILE]
            nc.sync.dma_start(out=dst.rearrange("(m p) t -> p m t", p=P), in_=result[c][:, m0 : m0 + count, :])

        def finish(c, m):
            silu(c, m)
            if c == CHUNKS - 1:
                store(c, m, 1)
            elif m % 4 == 3:
                store(c, m - 3, 4)

        def linears(i, c0=0, width=N_TILE):
            for m in range(M_TILES):
                linear(i, m, c0, width)

        def quadratics(i):
            for m in range(M_TILES):
                quadratic(i, m)

        for i in range(PASSES):
            square_scalar(i, 0, HALF)
            square_scalar(i, HALF, HALF)
            cast(i, 0, HALF)
            quantize("xb", i, 0, HALF)
            cast(i, HALF, HALF)
            quantize("xa", i, 0, HALF)
            quantize("xb", i, HALF, HALF)
            quantize("xa", i, HALF, HALF)
            linears(i, 0, HALF)
            if i < PASSES - 1:
                linears(i, HALF, HALF)
                quadratics(i)
        nc.vector.transpose(bias[:], bias_rows[:])
        square_scalar(3, 0, HALF)
        cast(3, 0, HALF)
        quantize("xb", 3, 0, HALF)
        cast(3, HALF, HALF)
        quantize("xa", 3, 0, HALF)
        quantize("xb", 3, HALF, HALF)
        multiply(2, LAG_CLOSE, HALF, HALF, after=lambda m: finish(0, m))
        linears(3)
        square_scalar(3, HALF, HALF)
        square_scalar(4, 0, HALF)
        square_scalar(5, 0, N_TILE)
        cast(4, 0, N_TILE)
        quantize("xb", 4, 0, N_TILE)
        square_flat(4, HALF, HALF)
        quantize("xa", 3, HALF, HALF)
        interleave_flat(4, HALF, HALF)
        cast(5, 0, N_TILE)
        quantize("xa", 4, HALF, HALF)
        quantize("xa", 4, 0, HALF)
        quantize("xb", 5, 0, N_TILE)
        quantize("xa", 5, 0, N_TILE)
        cast(6, 0, N_TILE)
        linears(4)
        quadratics(3)
        quadratics(4)
        multiply(5, 1, after=lambda m: finish(1, m))
        square_flat(6, 0, N_TILE)
        quantize("xb", 6, 0, N_TILE)
        interleave_flat(6, 0, N_TILE)
        quantize("xa", 6, 0, N_TILE)
        cast(7, 0, N_TILE)
        quantize("xb", 7, 0, N_TILE)
        square_scalar(7, 0, N_TILE)
        square_scalar(8, 0, N_TILE)
        cast(8, 0, N_TILE)
        quantize("xa", 7, 0, N_TILE)
        quantize("xb", 8, 0, N_TILE)
        quantize("xa", 8, 0, N_TILE)
        linears(6)
        quadratics(6)
        linears(7)
        for m in range(M_TILES):
            quadratic(7, m)
            linear(8, m)
            quadratic(8, m)
            finish(2, m)
